import numpy as np
import ml_dtypes


def mxq(x, axis, fmt="e4m3"):
    dtype, down = {"e4m3": (ml_dtypes.float8_e4m3fn, 7), "e5m2": (ml_dtypes.float8_e5m2, 14)}[fmt]
    v = np.moveaxis(np.asarray(x, np.float32).astype(ml_dtypes.bfloat16).astype(np.float64), axis, -1)
    blocks = v.reshape(v.shape[:-1] + (-1, 32))
    amax = np.abs(blocks).max(-1, keepdims=True)
    byte = np.maximum(np.where(amax > 0, np.frexp(amax)[1] - 1 + 127, 0) - down, 1)
    scale = np.exp2(byte - 127.0)
    codes = (blocks / scale).astype(np.float32).astype(dtype).astype(np.float64)
    return np.moveaxis((codes * scale).reshape(v.shape), -1, axis)


WIDE = False


def mx_kscale(k):
    if not WIDE:
        return np.ones(k)
    levels = np.array([10, -10, 5, -5, 0])
    if k % 512:
        return np.exp2(np.random.permutation(np.resize(levels, k // 32))).repeat(32)
    a = np.empty((k // 512, 16))
    for p in range(k // 512):
        a[p, :8] = np.random.permutation(np.resize(levels, 8))
        for g in range(8):
            far = levels[np.abs(levels - a[p, g]) >= 10]
            a[p, g + 8] = far[np.random.randint(len(far))]
    return np.exp2(a.ravel()).repeat(32)


def f64(x):
    return np.asarray(x).astype(np.float64)


def striped8(idx):
    return np.concatenate([v.reshape(-1, 16).T for v in idx]).astype(np.uint16)


def unstriped8(offs):
    return np.stack([offs[16 * g:16 * g + 16].T.reshape(-1) for g in range(8)]).astype(np.int64)


E2M1 = np.array([0.0, 0.5, 1.0, 1.5, 2.0, 3.0, 4.0, 6.0, -0.0, -0.5, -1.0, -1.5, -2.0, -3.0, -4.0, -6.0])


def pack_weight(w, fmt):
    k, n = w.shape
    w = f64(np.asarray(w, np.float32).astype(ml_dtypes.bfloat16)).reshape(k // 32, 32, n)
    amax = np.abs(w).max(1)
    if fmt == "e4m3":
        byte = np.frexp(amax)[1] - 1 + 127 - 7
    else:
        mant, ex = np.frexp(amax / 6.0)
        byte = np.where(mant > 0.5, ex, ex - 1) + 127
    byte = np.clip(np.where(amax > 0, byte, 1), 1, 254)
    scaled = (w * np.exp2(127.0 - byte)[:, None, :]).reshape(k, n).astype(np.float32)
    by_word = np.ascontiguousarray(scaled.reshape(k // 512, 128, 4, n).transpose(0, 1, 3, 2))
    if fmt == "e4m3":
        words = by_word.astype(ml_dtypes.float8_e4m3fn).view(np.uint8)
    else:
        c = by_word.astype(ml_dtypes.float4_e2m1fn).view(np.uint8) & 0xF
        words = (c[..., 0::2] | (c[..., 1::2] << 4)).reshape(k // 512, 128, 2 * n)
    return np.ascontiguousarray(words), np.ascontiguousarray(byte.astype(np.uint8).reshape(k // 512, 16, n))


def unpack_weight(words, scales, fmt):
    g, _, n = scales.shape
    words = np.ascontiguousarray(words).reshape(g, 128, n, -1)
    if fmt == "e4m3":
        vals = words.view(ml_dtypes.float8_e4m3fn).astype(np.float64)
    else:
        nib = np.empty((g, 128, n, 4), np.uint8)
        nib[..., 0::2] = words & 0xF
        nib[..., 1::2] = words >> 4
        vals = E2M1[nib]
    vals = vals * np.repeat(np.exp2(scales.astype(np.float64) - 127.0), 8, axis=1)[..., None]
    return vals.transpose(0, 1, 3, 2).reshape(g * 512, n)


def gelu(v):
    return 0.5 * v * (1.0 + np.tanh(np.sqrt(2.0 / np.pi) * (v + 0.044715 * v**3)))


K, M, T, S = 1536, 1024, 1024, 512


def setup_inputs():
    n = np.random.standard_normal
    s = mx_kscale(K)[:, None]
    p_w = pack_weight(n((K, M)) / np.sqrt(K) / s, "e4m3")
    return {
        "xT": (n((K, T)) * s).astype(np.float32),
        "w_words": p_w[0],
        "w_scales": p_w[1],
        "wgt": np.repeat(np.random.uniform(0.5, 2.0, (8, S)), 16, axis=0).astype(np.float32),
        "b": (0.3 * n(1024)).astype(np.float32),
        "wgo": np.repeat(np.random.uniform(0.5, 2.0, (8, S)), 16, axis=0).astype(np.float32),
        "offs": striped8(np.stack([np.random.permutation(T)[:S] for _ in range(8)])),
        "offs2": striped8(np.stack([np.random.permutation(T)[:S] for _ in range(8)])),
    }


def reference(xT, w_words, w_scales, wgt, b, wgo, offs, offs2):
    idx = unstriped8(offs)
    group = np.arange(K) % 512 // 64
    xg = f64(wgt)[np.arange(K) // 4 % 128] * f64(xT)[np.arange(K)[:, None], idx[group]]
    xT_ = mxq(xg, 0, "e4m3")
    w_ = unpack_weight(w_words, w_scales, "e4m3")
    y = w_.T @ xT_
    place = unstriped8(offs2)[np.arange(M) % 128 // 16]
    out = np.zeros((M, T))
    out[np.arange(M)[:, None], place] = f64(wgo)[np.arange(M) % 128] * (gelu(y + f64(b)[:, None]))
    return out

@@ -1,0 +1,160 @@
+from contextlib import ExitStack
+
+import concourse.mybir as mybir
+
+F32 = mybir.dt.float32
+BF16 = mybir.dt.bfloat16
+I32 = mybir.dt.int32
+U32 = mybir.dt.uint32
+U16 = mybir.dt.uint16
+U8 = mybir.dt.uint8
+FP8X4 = mybir.dt.float8_e4m3fn_x4
+MULT = mybir.AluOpType.mult
+GELU = mybir.ActivationFunctionType.Gelu_apprx_tanh
+
+K, M, T, S = 1536, 1024, 1024, 512
+P = 128
+PACK = 4
+PASSES = K // (P * PACK)
+ROW_TILES = M // P
+HALF = S // 2
+OFF_COLS = HALF // 16
+
+FLOPS = 2 * K * M * S
+
+
+def tile_list_hboth_gelu_kernel(tc, xT, w_words, w_scales, wgt, b, wgo, offs, offs2, out):
+    nc = tc.nc
+    with ExitStack() as ctx:
+        keep = ctx.enter_context(tc.tile_pool(name="keep", bufs=1))
+        psum = ctx.enter_context(tc.psum_pool(name="psum", bufs=8))
+
+        offs_sb = keep.tile([P, S // 16], U16, name="offs_sb")
+        offs2_sb = keep.tile([P, S // 16], U16, name="offs2_sb")
+        wgt_sb = [keep.tile([P, HALF], F32, name=f"wgt{h}") for h in range(2)]
+        wgo_sb = keep.tile([P, S], F32, name="wgo_sb")
+        x_sb = [[keep.tile([P, T], F32, name=f"x{a}_{i}") for i in range(PACK)] for a in range(PASSES)]
+        w_sb = [keep.tile([P, M], U32, align_bytes=64, name=f"w{a}") for a in range(PASSES)]
+        w_scale = keep.tile([P, M], U8, align_bytes=64, name="w_scale")
+        b_rows = keep.tile([P, 32], F32, align_bytes=64, name="b_rows")
+        b_col = keep.tile([P, 32], F32, align_bytes=64, name="b_col")
+        warm = keep.tile([P, 1], F32, name="warm")
+        windows = [keep.tile([P, T], F32, name=f"window{r}") for r in range(ROW_TILES)]
+        picked = [[keep.tile([P, PACK, HALF], F32, name=f"picked{a}_{h}") for h in range(2)] for a in range(PASSES)]
+        grouped = [keep.tile([P, S, PACK], BF16, align_bytes=64, name=f"grouped{a}") for a in range(PASSES)]
+        codes = [keep.tile([P, S], U32, align_bytes=64, name=f"codes{a}") for a in range(PASSES)]
+        scales = [keep.tile([P, S], U8, align_bytes=64, name=f"scales{a}") for a in range(PASSES)]
+        acted = [[keep.tile([P, HALF], F32, name=f"acted{r}_{h}") for h in range(2)] for r in range(ROW_TILES)]
+
+        def load_x(a, i):
+            rows = xT.rearrange("(a p i) t -> a i p t", a=PASSES, i=PACK)
+            nc.sync.dma_start(x_sb[a][i][:], rows[a, i])
+
+        nc.vector.memset(warm[:], 0.0)
+        nc.vector.memset(b_rows[:], 0.0)
+        nc.vector.memset(w_scale[:].bitcast(I32), 0)
+        nc.sync.dma_start(offs_sb[:], offs)
+        nc.scalar.dma_start(wgt_sb[0][:], wgt[:, 0:HALF])
+        load_x(0, 0)
+        nc.scalar.dma_start(wgt_sb[1][:], wgt[:, HALF:S])
+        nc.scalar.activation(warm[:], warm[:], GELU)
+        for r in range(ROW_TILES):
+            engine = nc.gpsimd if r % 3 == 2 else nc.vector
+            engine.memset(windows[r][:], 0.0)
+        load_x(0, 1)
+        load_x(0, 2)
+        load_x(0, 3)
+        b_view = b.rearrange("(r q i) -> q r i", q=4, i=32)
+        for q in range(4):
+            nc.sync.dma_start(b_rows[32 * q : 32 * q + ROW_TILES, :], b_view[q])
+        for i in range(PACK):
+            load_x(1, i)
+        for q in range(4):
+            nc.sync.dma_start(
+                w_scale[32 * q : 32 * q + 4 * PASSES, :].bitcast(I32),
+                w_scales[:, 4 * q : 4 * q + 4, :].bitcast(I32),
+            )
+        for i in range(PACK):
+            load_x(2, i)
+        for a in range(PASSES):
+            nc.sync.dma_start(w_sb[a][:].bitcast(I32), w_words[a].rearrange("p n i -> p (n i)").bitcast(I32))
+        nc.sync.dma_start(offs2_sb[:], offs2)
+        nc.sync.dma_start(wgo_sb[:], wgo)
+
+        def gather(a, i, h):
+            nc.vector.tensor_tensor(
+                picked[a][h][:, i, :],
+                x_sb[a][i][:].indirect(offs_sb[:, h * OFF_COLS : (h + 1) * OFF_COLS]),
+                wgt_sb[h][:],
+                MULT,
+            )
+
+        def interleave(a, h):
+            nc.scalar.copy(
+                out=grouped[a][:, h * HALF : (h + 1) * HALF, :].rearrange("p (c i) t -> p c t i", i=4),
+                in_=picked[a][h][:].rearrange("p t (c i) -> p c t i", i=4),
+            )
+
+        def quantize(a, first, last):
+            nc.vector.quantize_mx(
+                out=codes[a][:, first:last].bitcast(FP8X4),
+                scales=scales[a][:, first:last],
+                in_=grouped[a][:, first:last, :].rearrange("p c t -> p (c t)"),
+            )
+
+        def project(r, h):
+            acc = psum.tile([P, 512], F32, name="acc")
+            cols = slice(r * P, (r + 1) * P)
+            for a in range(PASSES):
+                nc.tensor.matmul_mx(
+                    out=acc[:, 0:HALF],
+                    lhsT=w_sb[a][:, cols].bitcast(FP8X4),
+                    lhsT_scale=w_scale[4 * a :, cols],
+                    rhs=codes[a][:, h * HALF : (h + 1) * HALF].bitcast(FP8X4),
+                    rhs_scale=scales[a][:, h * HALF : (h + 1) * HALF],
+                    start=(a == 0),
+                    stop=(a == PASSES - 1),
+                )
+            nc.scalar.activation(acted[r][h][:], acc[:, 0:HALF], GELU, bias=b_col[:, r : r + 1])
+
+        def scatter(r, h):
+            nc.vector.tensor_tensor(
+                windows[r][:].indirect(offs2_sb[:, h * OFF_COLS : (h + 1) * OFF_COLS]),
+                acted[r][h][:],
+                wgo_sb[:, h * HALF : (h + 1) * HALF],
+                MULT,
+            )
+
+        for i in range(PACK):
+            gather(0, i, 0)
+            gather(0, i, 1)
+        interleave(0, 0)
+        interleave(0, 1)
+        for i in range(PACK):
+            gather(1, i, 0)
+            gather(1, i, 1)
+        interleave(1, 0)
+        interleave(1, 1)
+        quantize(0, 0, S)
+        nc.vector.transpose(b_col[:], b_rows[:])
+        for i in range(PACK):
+            gather(2, i, 0)
+        interleave(2, 0)
+        quantize(1, 0, S)
+        gather(2, 0, 1)
+        gather(2, 1, 1)
+        quantize(2, 0, HALF)
+        gather(2, 2, 1)
+        gather(2, 3, 1)
+        interleave(2, 1)
+        for r in range(ROW_TILES):
+            project(r, 0)
+        scatter(0, 0)
+        quantize(2, HALF, S)
+        for r in range(1, ROW_TILES):
+            scatter(r, 0)
+        for r in range(ROW_TILES):
+            project(r, 1)
+        for r in range(ROW_TILES):
+            scatter(r, 1)
+            nc.sync.dma_start(out[r * P : (r + 1) * P, :], windows[r][:])

@@ -17,6 +17,7 @@ P = 128
 PACK = 4
 PASSES = K // (P * PACK)
 ROW_TILES = M // P
+WINDOWS = 4
 HALF = S // 2
 OFF_COLS = HALF // 16
 
@@ -39,7 +40,7 @@ def tile_list_hboth_gelu_kernel(tc, xT, w_words, w_scales, wgt, b, wgo, offs, of
         b_rows = keep.tile([P, 32], F32, align_bytes=64, name="b_rows")
         b_col = keep.tile([P, 32], F32, align_bytes=64, name="b_col")
         warm = keep.tile([P, 1], F32, name="warm")
-        windows = [keep.tile([P, T], F32, name=f"window{r}") for r in range(ROW_TILES)]
+        windows = [keep.tile([P, T], F32, name=f"window{r}") for r in range(WINDOWS)]
         picked = [[keep.tile([P, PACK, HALF], F32, name=f"picked{a}_{h}") for h in range(2)] for a in range(PASSES)]
         grouped = [keep.tile([P, S, PACK], BF16, align_bytes=64, name=f"grouped{a}") for a in range(PASSES)]
         codes = [keep.tile([P, S], U32, align_bytes=64, name=f"codes{a}") for a in range(PASSES)]
@@ -58,8 +59,8 @@ def tile_list_hboth_gelu_kernel(tc, xT, w_words, w_scales, wgt, b, wgo, offs, of
         load_x(0, 0)
         nc.scalar.dma_start(wgt_sb[1][:], wgt[:, HALF:S])
         nc.scalar.activation(warm[:], warm[:], GELU)
-        for r in range(ROW_TILES):
-            engine = nc.gpsimd if r % 3 == 2 else nc.vector
+        for r in range(WINDOWS):
+            engine = nc.vector if r % 2 == 0 else nc.gpsimd
             engine.memset(windows[r][:], 0.0)
         load_x(0, 1)
         load_x(0, 2)
@@ -119,7 +120,7 @@ def tile_list_hboth_gelu_kernel(tc, xT, w_words, w_scales, wgt, b, wgo, offs, of
 
         def scatter(r, h):
             nc.vector.tensor_tensor(
-                windows[r][:].indirect(offs2_sb[:, h * OFF_COLS : (h + 1) * OFF_COLS]),
+                windows[r % WINDOWS][:].indirect(offs2_sb[:, h * OFF_COLS : (h + 1) * OFF_COLS]),
                 acted[r][h][:],
                 wgo_sb[:, h * HALF : (h + 1) * HALF],
                 MULT,
@@ -132,10 +133,11 @@ def tile_list_hboth_gelu_kernel(tc, xT, w_words, w_scales, wgt, b, wgo, offs, of
         interleave(0, 1)
         for i in range(PACK):
             gather(1, i, 0)
-            gather(1, i, 1)
         interleave(1, 0)
-        interleave(1, 1)
         quantize(0, 0, S)
+        for i in range(PACK):
+            gather(1, i, 1)
+        interleave(1, 1)
         nc.vector.transpose(b_col[:], b_rows[:])
         for i in range(PACK):
             gather(2, i, 0)
@@ -144,17 +146,20 @@ def tile_list_hboth_gelu_kernel(tc, xT, w_words, w_scales, wgt, b, wgo, offs, of
         gather(2, 0, 1)
         gather(2, 1, 1)
         quantize(2, 0, HALF)
+        project(0, 0)
+        project(1, 0)
         gather(2, 2, 1)
         gather(2, 3, 1)
         interleave(2, 1)
-        for r in range(ROW_TILES):
-            project(r, 0)
         scatter(0, 0)
+        project(2, 0)
+        scatter(1, 0)
         quantize(2, HALF, S)
-        for r in range(1, ROW_TILES):
-            scatter(r, 0)
+        scatter(2, 0)
         for r in range(ROW_TILES):
             project(r, 1)
-        for r in range(ROW_TILES):
+            if r > 2:
+                project(r, 0)
+                scatter(r, 0)
             scatter(r, 1)
-            nc.sync.dma_start(out[r * P : (r + 1) * P, :], windows[r][:])
+            nc.sync.dma_start(out[r * P : (r + 1) * P, :], windows[r % WINDOWS][:])

@@ -54,28 +54,28 @@ def tile_list_hboth_gelu_kernel(tc, xT, w_words, w_scales, wgt, b, wgo, offs, of
         nc.vector.memset(warm[:], 0.0)
         nc.vector.memset(b_rows[:], 0.0)
         nc.vector.memset(w_scale[:].bitcast(I32), 0)
-        nc.sync.dma_start(offs_sb[:], offs)
-        nc.scalar.dma_start(wgt_sb[0][:], wgt[:, 0:HALF])
-        load_x(0, 0)
-        nc.scalar.dma_start(wgt_sb[1][:], wgt[:, HALF:S])
-        nc.scalar.activation(warm[:], warm[:], GELU)
-        for r in range(WINDOWS):
-            engine = nc.vector if r % 2 == 0 else nc.gpsimd
-            engine.memset(windows[r][:], 0.0)
-        load_x(0, 1)
-        load_x(0, 2)
-        load_x(0, 3)
+        for window in windows:
+            nc.vector.memset(window[:].bitcast(I32), 0)
         b_view = b.rearrange("(r q i) -> q r i", q=4, i=32)
         for q in range(4):
-            nc.sync.dma_start(b_rows[32 * q : 32 * q + ROW_TILES, :], b_view[q])
+            nc.scalar.dma_start(b_rows[32 * q : 32 * q + ROW_TILES, :], b_view[q])
+        nc.scalar.activation(warm[:], warm[:], GELU)
+
+        nc.sync.dma_start(offs_sb[:], offs)
+        nc.sync.dma_start(wgt_sb[0][:], wgt[:, 0:HALF])
+        load_x(0, 0)
+        nc.sync.dma_start(wgt_sb[1][:], wgt[:, HALF:S])
+        for i in range(1, PACK):
+            load_x(0, i)
         for i in range(PACK):
             load_x(1, i)
+        load_x(2, 0)
         for q in range(4):
             nc.sync.dma_start(
                 w_scale[32 * q : 32 * q + 4 * PASSES, :].bitcast(I32),
                 w_scales[:, 4 * q : 4 * q + 4, :].bitcast(I32),
             )
-        for i in range(PACK):
+        for i in range(1, PACK):
             load_x(2, i)
         for a in range(PASSES):
             nc.sync.dma_start(w_sb[a][:].bitcast(I32), w_words[a].rearrange("p n i -> p (n i)").bitcast(I32))
@@ -126,6 +126,9 @@ def tile_list_hboth_gelu_kernel(tc, xT, w_words, w_scales, wgt, b, wgo, offs, of
                 MULT,
             )
 
+        def store(r):
+            nc.sync.dma_start(out[r * P : (r + 1) * P, :], windows[r % WINDOWS][:])
+
         for i in range(PACK):
             gather(0, i, 0)
             gather(0, i, 1)
@@ -153,13 +156,30 @@ def tile_list_hboth_gelu_kernel(tc, xT, w_words, w_scales, wgt, b, wgo, offs, of
         interleave(2, 1)
         scatter(0, 0)
         project(2, 0)
+        project(3, 0)
         scatter(1, 0)
         quantize(2, HALF, S)
+        project(0, 1)
+        project(1, 1)
         scatter(2, 0)
-        for r in range(ROW_TILES):
-            project(r, 1)
-            if r > 2:
-                project(r, 0)
-                scatter(r, 0)
+        scatter(3, 0)
+        scatter(0, 1)
+        store(0)
+        scatter(1, 1)
+        store(1)
+        project(2, 1)
+        project(3, 1)
+        scatter(2, 1)
+        store(2)
+        scatter(3, 1)
+        store(3)
+        for r in range(4, ROW_TILES, 2):
+            for h in range(2):
+                project(r, h)
+                project(r + 1, h)
+            scatter(r, 0)
+            scatter(r + 1, 0)
             scatter(r, 1)
-            nc.sync.dma_start(out[r * P : (r + 1) * P, :], windows[r % WINDOWS][:])
+            store(r)
+            scatter(r + 1, 1)
+            store(r + 1)

@@ -33,9 +33,9 @@ def tile_list_hboth_gelu_kernel(tc, xT, w_words, w_scales, wgt, b, wgo, offs, of
         offs_sb = keep.tile([P, S // 16], U16, name="offs_sb")
         offs2_sb = keep.tile([P, S // 16], U16, name="offs2_sb")
         wgt_sb = [keep.tile([P, HALF], F32, name=f"wgt{h}") for h in range(2)]
-        wgo_sb = keep.tile([P, S], F32, name="wgo_sb")
+        wgo_sb = [keep.tile([P, HALF], F32, name=f"wgo{h}") for h in range(2)]
         x_sb = [[keep.tile([P, T], F32, name=f"x{a}_{i}") for i in range(PACK)] for a in range(PASSES)]
-        w_sb = [keep.tile([P, M], U32, align_bytes=64, name=f"w{a}") for a in range(PASSES)]
+        w_sb = [[keep.tile([P, M // 2], U32, align_bytes=64, name=f"w{a}_{part}") for part in range(2)] for a in range(PASSES)]
         w_scale = keep.tile([P, M], U8, align_bytes=64, name="w_scale")
         b_rows = keep.tile([P, 32], F32, align_bytes=64, name="b_rows")
         b_col = keep.tile([P, 32], F32, align_bytes=64, name="b_col")
@@ -77,10 +77,16 @@ def tile_list_hboth_gelu_kernel(tc, xT, w_words, w_scales, wgt, b, wgo, offs, of
             )
         for i in range(1, PACK):
             load_x(2, i)
-        for a in range(PASSES):
-            nc.sync.dma_start(w_sb[a][:].bitcast(I32), w_words[a].rearrange("p n i -> p (n i)").bitcast(I32))
-        nc.sync.dma_start(offs2_sb[:], offs2)
-        nc.sync.dma_start(wgo_sb[:], wgo)
+        for part in range(2):
+            cols = slice(part * M // 2, (part + 1) * M // 2)
+            for a in range(PASSES):
+                nc.sync.dma_start(
+                    w_sb[a][part][:].bitcast(I32),
+                    w_words[a, :, cols, :].rearrange("p n i -> p (n i)").bitcast(I32),
+                )
+            if part == 0:
+                nc.sync.dma_start(offs2_sb[:], offs2)
+            nc.sync.dma_start(wgo_sb[part][:], wgo[:, part * HALF : (part + 1) * HALF])
 
         def gather(a, i, h):
             nc.vector.tensor_tensor(
@@ -106,10 +112,11 @@ def tile_list_hboth_gelu_kernel(tc, xT, w_words, w_scales, wgt, b, wgo, offs, of
         def project(r, h):
             acc = psum.tile([P, 512], F32, name="acc")
             cols = slice(r * P, (r + 1) * P)
+            part, first = divmod(r * P, M // 2)
             for a in range(PASSES):
                 nc.tensor.matmul_mx(
                     out=acc[:, 0:HALF],
-                    lhsT=w_sb[a][:, cols].bitcast(FP8X4),
+                    lhsT=w_sb[a][part][:, first : first + P].bitcast(FP8X4),
                     lhsT_scale=w_scale[4 * a :, cols],
                     rhs=codes[a][:, h * HALF : (h + 1) * HALF].bitcast(FP8X4),
                     rhs_scale=scales[a][:, h * HALF : (h + 1) * HALF],
@@ -122,7 +129,7 @@ def tile_list_hboth_gelu_kernel(tc, xT, w_words, w_scales, wgt, b, wgo, offs, of
             nc.vector.tensor_tensor(
                 windows[r % WINDOWS][:].indirect(offs2_sb[:, h * OFF_COLS : (h + 1) * OFF_COLS]),
                 acted[r][h][:],
-                wgo_sb[:, h * HALF : (h + 1) * HALF],
+                wgo_sb[h][:],
                 MULT,
             )
 

@@ -45,17 +45,21 @@ def tile_list_hboth_gelu_kernel(tc, xT, w_words, w_scales, wgt, b, wgo, offs, of
         grouped = [keep.tile([P, S, PACK], BF16, align_bytes=64, name=f"grouped{a}") for a in range(PASSES)]
         codes = [keep.tile([P, S], U32, align_bytes=64, name=f"codes{a}") for a in range(PASSES)]
         scales = [keep.tile([P, S], U8, align_bytes=64, name=f"scales{a}") for a in range(PASSES)]
-        acted = [[keep.tile([P, HALF], F32, name=f"acted{r}_{h}") for h in range(2)] for r in range(ROW_TILES)]
+        acted = [keep.tile([P, S], F32, name=f"acted{r}") for r in range(ROW_TILES)]
 
         def load_x(a, i):
             rows = xT.rearrange("(a p i) t -> a i p t", a=PASSES, i=PACK)
             nc.sync.dma_start(x_sb[a][i][:], rows[a, i])
 
+        def load_wgo(h):
+            nc.sync.dma_start(wgo_sb[h][:], wgo[:, h * HALF : (h + 1) * HALF])
+
         nc.vector.memset(warm[:], 0.0)
         nc.vector.memset(b_rows[:], 0.0)
         nc.vector.memset(w_scale[:].bitcast(I32), 0)
-        for window in windows:
-            nc.vector.memset(window[:].bitcast(I32), 0)
+        for i, window in enumerate(windows):
+            engine = nc.vector if i < 2 else nc.gpsimd
+            engine.memset(window[:].bitcast(I32), 0)
         b_view = b.rearrange("(r q i) -> q r i", q=4, i=32)
         for q in range(4):
             nc.scalar.dma_start(b_rows[32 * q : 32 * q + ROW_TILES, :], b_view[q])
@@ -70,13 +74,15 @@ def tile_list_hboth_gelu_kernel(tc, xT, w_words, w_scales, wgt, b, wgo, offs, of
         for i in range(PACK):
             load_x(1, i)
         load_x(2, 0)
+        nc.sync.dma_start(offs2_sb[:], offs2)
+        load_wgo(0)
+        for i in range(1, PACK):
+            load_x(2, i)
         for q in range(4):
             nc.sync.dma_start(
                 w_scale[32 * q : 32 * q + 4 * PASSES, :].bitcast(I32),
                 w_scales[:, 4 * q : 4 * q + 4, :].bitcast(I32),
             )
-        for i in range(1, PACK):
-            load_x(2, i)
         for part in range(2):
             cols = slice(part * M // 2, (part + 1) * M // 2)
             for a in range(PASSES):
@@ -84,9 +90,7 @@ def tile_list_hboth_gelu_kernel(tc, xT, w_words, w_scales, wgt, b, wgo, offs, of
                     w_sb[a][part][:].bitcast(I32),
                     w_words[a, :, cols, :].rearrange("p n i -> p (n i)").bitcast(I32),
                 )
-            if part == 0:
-                nc.sync.dma_start(offs2_sb[:], offs2)
-            nc.sync.dma_start(wgo_sb[part][:], wgo[:, part * HALF : (part + 1) * HALF])
+        load_wgo(1)
 
         def gather(a, i, h):
             nc.vector.tensor_tensor(
@@ -109,26 +113,26 @@ def tile_list_hboth_gelu_kernel(tc, xT, w_words, w_scales, wgt, b, wgo, offs, of
                 in_=grouped[a][:, first:last, :].rearrange("p c t -> p (c t)"),
             )
 
-        def project(r, h):
-            acc = psum.tile([P, 512], F32, name="acc")
+        def project(r, first, last):
+            acc = psum.tile([P, S], F32, name="acc")
             cols = slice(r * P, (r + 1) * P)
-            part, first = divmod(r * P, M // 2)
+            part, w_first = divmod(r * P, M // 2)
             for a in range(PASSES):
                 nc.tensor.matmul_mx(
-                    out=acc[:, 0:HALF],
-                    lhsT=w_sb[a][part][:, first : first + P].bitcast(FP8X4),
+                    out=acc[:, first:last],
+                    lhsT=w_sb[a][part][:, w_first : w_first + P].bitcast(FP8X4),
                     lhsT_scale=w_scale[4 * a :, cols],
-                    rhs=codes[a][:, h * HALF : (h + 1) * HALF].bitcast(FP8X4),
-                    rhs_scale=scales[a][:, h * HALF : (h + 1) * HALF],
+                    rhs=codes[a][:, first:last].bitcast(FP8X4),
+                    rhs_scale=scales[a][:, first:last],
                     start=(a == 0),
                     stop=(a == PASSES - 1),
                 )
-            nc.scalar.activation(acted[r][h][:], acc[:, 0:HALF], GELU, bias=b_col[:, r : r + 1])
+            nc.scalar.activation(acted[r][:, first:last], acc[:, first:last], GELU, bias=b_col[:, r : r + 1])
 
         def scatter(r, h):
             nc.vector.tensor_tensor(
                 windows[r % WINDOWS][:].indirect(offs2_sb[:, h * OFF_COLS : (h + 1) * OFF_COLS]),
-                acted[r][h][:],
+                acted[r][:, h * HALF : (h + 1) * HALF],
                 wgo_sb[h][:],
                 MULT,
             )
@@ -156,34 +160,33 @@ def tile_list_hboth_gelu_kernel(tc, xT, w_words, w_scales, wgt, b, wgo, offs, of
         gather(2, 0, 1)
         gather(2, 1, 1)
         quantize(2, 0, HALF)
-        project(0, 0)
-        project(1, 0)
+        project(0, 0, HALF)
+        project(1, 0, HALF)
         gather(2, 2, 1)
         gather(2, 3, 1)
         interleave(2, 1)
         scatter(0, 0)
-        project(2, 0)
-        project(3, 0)
+        project(2, 0, HALF)
+        project(3, 0, HALF)
         scatter(1, 0)
         quantize(2, HALF, S)
-        project(0, 1)
-        project(1, 1)
+        project(0, HALF, S)
+        project(1, HALF, S)
         scatter(2, 0)
         scatter(3, 0)
         scatter(0, 1)
         store(0)
         scatter(1, 1)
         store(1)
-        project(2, 1)
-        project(3, 1)
+        project(2, HALF, S)
+        project(3, HALF, S)
         scatter(2, 1)
         store(2)
         scatter(3, 1)
         store(3)
         for r in range(4, ROW_TILES, 2):
-            for h in range(2):
-                project(r, h)
-                project(r + 1, h)
+            project(r, 0, S)
+            project(r + 1, 0, S)
             scatter(r, 0)
             scatter(r + 1, 0)
             scatter(r, 1)

from contextlib import ExitStack

import concourse.mybir as mybir

F32 = mybir.dt.float32
BF16 = mybir.dt.bfloat16
I32 = mybir.dt.int32
U32 = mybir.dt.uint32
U16 = mybir.dt.uint16
U8 = mybir.dt.uint8
FP8X4 = mybir.dt.float8_e4m3fn_x4
MULT = mybir.AluOpType.mult
GELU = mybir.ActivationFunctionType.Gelu_apprx_tanh

K, M, T, S = 1536, 1024, 1024, 512
P = 128
PACK = 4
PASSES = K // (P * PACK)
ROW_TILES = M // P
WINDOWS = 4
HALF = S // 2
OFF_COLS = HALF // 16

FLOPS = 2 * K * M * S


def tile_list_hboth_gelu_kernel(tc, xT, w_words, w_scales, wgt, b, wgo, offs, offs2, out):
    nc = tc.nc
    with ExitStack() as ctx:
        keep = ctx.enter_context(tc.tile_pool(name="keep", bufs=1))
        psum = ctx.enter_context(tc.psum_pool(name="psum", bufs=8))

        offs_sb = keep.tile([P, S // 16], U16, name="offs_sb")
        offs2_sb = keep.tile([P, S // 16], U16, name="offs2_sb")
        wgt_sb = [keep.tile([P, HALF], F32, name=f"wgt{h}") for h in range(2)]
        wgo_sb = [keep.tile([P, HALF], F32, name=f"wgo{h}") for h in range(2)]
        x_sb = [[keep.tile([P, T], F32, name=f"x{a}_{i}") for i in range(PACK)] for a in range(PASSES)]
        w_sb = [[keep.tile([P, M // 2], U32, align_bytes=64, name=f"w{a}_{part}") for part in range(2)] for a in range(PASSES)]
        w_scale = keep.tile([P, M], U8, align_bytes=64, name="w_scale")
        b_rows = keep.tile([P, 32], F32, align_bytes=64, name="b_rows")
        b_col = keep.tile([P, 32], F32, align_bytes=64, name="b_col")
        warm = keep.tile([P, 1], F32, name="warm")
        windows = [keep.tile([P, T], F32, name=f"window{r}") for r in range(WINDOWS)]
        picked = [[keep.tile([P, PACK, HALF], F32, name=f"picked{a}_{h}") for h in range(2)] for a in range(PASSES)]
        grouped = [keep.tile([P, S, PACK], BF16, align_bytes=64, name=f"grouped{a}") for a in range(PASSES)]
        codes = [keep.tile([P, S], U32, align_bytes=64, name=f"codes{a}") for a in range(PASSES)]
        scales = [keep.tile([P, S], U8, align_bytes=64, name=f"scales{a}") for a in range(PASSES)]
        acted = [keep.tile([P, S], F32, name=f"acted{r}") for r in range(ROW_TILES)]

        def load_x(a, i):
            rows = xT.rearrange("(a p i) t -> a i p t", a=PASSES, i=PACK)
            nc.sync.dma_start(x_sb[a][i][:], rows[a, i])

        def load_wgo(h):
            nc.sync.dma_start(wgo_sb[h][:], wgo[:, h * HALF : (h + 1) * HALF])

        nc.vector.memset(warm[:], 0.0)
        nc.vector.memset(b_rows[:], 0.0)
        nc.vector.memset(w_scale[:].bitcast(I32), 0)
        for i, window in enumerate(windows):
            engine = nc.vector if i < 2 else nc.gpsimd
            engine.memset(window[:].bitcast(I32), 0)
        b_view = b.rearrange("(r q i) -> q r i", q=4, i=32)
        for q in range(4):
            nc.scalar.dma_start(b_rows[32 * q : 32 * q + ROW_TILES, :], b_view[q])
        nc.scalar.activation(warm[:], warm[:], GELU)

        nc.sync.dma_start(offs_sb[:], offs)
        nc.sync.dma_start(wgt_sb[0][:], wgt[:, 0:HALF])
        load_x(0, 0)
        nc.sync.dma_start(wgt_sb[1][:], wgt[:, HALF:S])
        for i in range(1, PACK):
            load_x(0, i)
        for i in range(PACK):
            load_x(1, i)
        load_x(2, 0)
        nc.sync.dma_start(offs2_sb[:], offs2)
        load_wgo(0)
        for i in range(1, PACK):
            load_x(2, i)
        for q in range(4):
            nc.sync.dma_start(
                w_scale[32 * q : 32 * q + 4 * PASSES, :].bitcast(I32),
                w_scales[:, 4 * q : 4 * q + 4, :].bitcast(I32),
            )
        for part in range(2):
            cols = slice(part * M // 2, (part + 1) * M // 2)
            for a in range(PASSES):
                nc.sync.dma_start(
                    w_sb[a][part][:].bitcast(I32),
                    w_words[a, :, cols, :].rearrange("p n i -> p (n i)").bitcast(I32),
                )
        load_wgo(1)

        def gather(a, i, h):
            nc.vector.tensor_tensor(
                picked[a][h][:, i, :],
                x_sb[a][i][:].indirect(offs_sb[:, h * OFF_COLS : (h + 1) * OFF_COLS]),
                wgt_sb[h][:],
                MULT,
            )

        def interleave(a, h):
            nc.scalar.copy(
                out=grouped[a][:, h * HALF : (h + 1) * HALF, :].rearrange("p (c i) t -> p c t i", i=4),
                in_=picked[a][h][:].rearrange("p t (c i) -> p c t i", i=4),
            )

        def quantize(a, first, last):
            nc.vector.quantize_mx(
                out=codes[a][:, first:last].bitcast(FP8X4),
                scales=scales[a][:, first:last],
                in_=grouped[a][:, first:last, :].rearrange("p c t -> p (c t)"),
            )

        def project(r, first, last):
            acc = psum.tile([P, S], F32, name="acc")
            cols = slice(r * P, (r + 1) * P)
            part, w_first = divmod(r * P, M // 2)
            for a in range(PASSES):
                nc.tensor.matmul_mx(
                    out=acc[:, first:last],
                    lhsT=w_sb[a][part][:, w_first : w_first + P].bitcast(FP8X4),
                    lhsT_scale=w_scale[4 * a :, cols],
                    rhs=codes[a][:, first:last].bitcast(FP8X4),
                    rhs_scale=scales[a][:, first:last],
                    start=(a == 0),
                    stop=(a == PASSES - 1),
                )
            nc.scalar.activation(acted[r][:, first:last], acc[:, first:last], GELU, bias=b_col[:, r : r + 1])

        def scatter(r, h):
            nc.vector.tensor_tensor(
                windows[r % WINDOWS][:].indirect(offs2_sb[:, h * OFF_COLS : (h + 1) * OFF_COLS]),
                acted[r][:, h * HALF : (h + 1) * HALF],
                wgo_sb[h][:],
                MULT,
            )

        def store(r):
            nc.sync.dma_start(out[r * P : (r + 1) * P, :], windows[r % WINDOWS][:])

        for i in range(PACK):
            gather(0, i, 0)
            gather(0, i, 1)
        interleave(0, 0)
        interleave(0, 1)
        for i in range(PACK):
            gather(1, i, 0)
        interleave(1, 0)
        quantize(0, 0, S)
        for i in range(PACK):
            gather(1, i, 1)
        interleave(1, 1)
        nc.vector.transpose(b_col[:], b_rows[:])
        for i in range(PACK):
            gather(2, i, 0)
        interleave(2, 0)
        quantize(1, 0, S)
        gather(2, 0, 1)
        gather(2, 1, 1)
        quantize(2, 0, HALF)
        project(0, 0, HALF)
        project(1, 0, HALF)
        gather(2, 2, 1)
        gather(2, 3, 1)
        interleave(2, 1)
        scatter(0, 0)
        project(2, 0, HALF)
        project(3, 0, HALF)
        scatter(1, 0)
        quantize(2, HALF, S)
        project(0, HALF, S)
        project(1, HALF, S)
        scatter(2, 0)
        scatter(3, 0)
        scatter(0, 1)
        store(0)
        scatter(1, 1)
        store(1)
        project(2, HALF, S)
        project(3, HALF, S)
        scatter(2, 1)
        store(2)
        scatter(3, 1)
        store(3)
        for r in range(4, ROW_TILES, 2):
            project(r, 0, S)
            project(r + 1, 0, S)
            scatter(r, 0)
            scatter(r + 1, 0)
            scatter(r, 1)
            store(r)
            scatter(r + 1, 1)
            store(r + 1)
